import numpy as np
import ml_dtypes

BF16 = ml_dtypes.bfloat16


def bf(x):
    return np.asarray(x, np.float32).astype(BF16)


def f32(x):
    return np.asarray(x, np.float32)


def f64(x):
    return np.asarray(x).astype(np.float64)


def striped(idx):
    return np.concatenate([l.reshape(-1, 16).T for l in idx])


def rows(idx, k):
    return np.tile(np.repeat(idx, 16, axis=0), (k // (16 * 8), 1))


def look(tab, idx):
    return np.take_along_axis(f64(tab), rows(idx, len(tab)), axis=1)


K, S, V, N, M = 128, 2048, 512, 512, 256


def setup_inputs():
    return {"tab": f32(np.random.standard_normal((K, S))), "y": f32(np.random.standard_normal((K, V))), "w": bf(np.random.standard_normal((K, M)) / np.sqrt(K)), "b": f32(0.5 * np.random.standard_normal((M, 1))), "offs": striped(np.stack([np.random.permutation(S)[:N] for _ in range(8)]))}


def reference(tab, y, w, b, offs):
    idx = np.stack([g.T.reshape(-1) for g in np.split(offs, 8)])
    t = look(tab, idx)
    x = np.tanh(t) * f64(y)
    y = f64(w).T @ x
    return np.maximum(y + f64(b), 0.0)

@@ -1,0 +1,48 @@
+import concourse.mybir as mybir
+
+F32, BF16, U16 = mybir.dt.float32, mybir.dt.bfloat16, mybir.dt.uint16
+ADD, MAX, MULT = mybir.AluOpType.add, mybir.AluOpType.max, mybir.AluOpType.mult
+TANH, RELU = mybir.ActivationFunctionType.Tanh, mybir.ActivationFunctionType.Relu
+
+P = 128
+S = 2048
+N = 512
+M = 256
+FLOPS = 2 * P * M * N
+BYTES = 4 * P * S + 4 * P * N + 2 * P * M + 4 * M + 2 * P * (N // 16) + 4 * M * N
+
+
+def tile_lookup_gate_tanh_relu_kernel(tc, tab, y, w, b, offs, out):
+    nc = tc.nc
+    with (
+        tc.tile_pool(name="held", bufs=1) as held,
+        tc.psum_pool(name="psum", bufs=1) as psum,
+    ):
+        offsets = held.tile([P, N // 16], U16, name="offsets")
+        nc.sync.dma_start(offsets[:], offs)
+        table = held.tile([P, S], F32, name="table")
+        nc.sync.dma_start(table[:], tab)
+        stream = held.tile([P, N], F32, name="stream")
+        nc.sync.dma_start(stream[:], y)
+        weights = held.tile([P, M], BF16, name="weights")
+        nc.sync.dma_start(weights[:], w)
+        bias = held.tile([P, M // P], F32, name="bias")
+        with nc.allow_non_contiguous_dma(reason="256 single float32 values, one to a partition and half"):
+            nc.scalar.dma_start(bias[:], b.rearrange("(h p) one -> p (h one)", p=P))
+
+        gate = held.tile([P, N], F32, name="gate")
+        nc.scalar.activation(gate[:], table[:].indirect(offsets[:]), TANH)
+
+        x = held.tile([P, N], BF16, name="x")
+        nc.vector.tensor_tensor(x[:], gate[:], stream[:], MULT)
+
+        for h in range(M // P):
+            product = psum.tile([P, N], F32, name=f"product{h}")
+            nc.tensor.matmul(product[:], weights[:, h * P : (h + 1) * P], x[:], start=True, stop=True)
+            result = held.tile([P, N], F32, name=f"result{h}")
+            if h == 0:
+                nc.vector.tensor_scalar(result[:], product[:], bias[:, h : h + 1], 0.0, ADD, MAX)
+                nc.sync.dma_start(out[h * P : (h + 1) * P, :], result[:])
+            else:
+                nc.scalar.activation(result[:], product[:], RELU, bias=bias[:, h : h + 1])
+                nc.scalar.dma_start(out[h * P : (h + 1) * P, :], result[:])

@@ -8,6 +8,7 @@ P = 128
 S = 2048
 N = 512
 M = 256
+C = N // 2
 FLOPS = 2 * P * M * N
 BYTES = 4 * P * S + 4 * P * N + 2 * P * M + 4 * M + 2 * P * (N // 16) + 4 * M * N
 
@@ -33,16 +34,18 @@ def tile_lookup_gate_tanh_relu_kernel(tc, tab, y, w, b, offs, out):
         gate = held.tile([P, N], F32, name="gate")
         nc.scalar.activation(gate[:], table[:].indirect(offsets[:]), TANH)
 
-        x = held.tile([P, N], BF16, name="x")
-        nc.vector.tensor_tensor(x[:], gate[:], stream[:], MULT)
-
-        for h in range(M // P):
-            product = psum.tile([P, N], F32, name=f"product{h}")
-            nc.tensor.matmul(product[:], weights[:, h * P : (h + 1) * P], x[:], start=True, stop=True)
-            result = held.tile([P, N], F32, name=f"result{h}")
-            if h == 0:
-                nc.vector.tensor_scalar(result[:], product[:], bias[:, h : h + 1], 0.0, ADD, MAX)
-                nc.sync.dma_start(out[h * P : (h + 1) * P, :], result[:])
-            else:
-                nc.scalar.activation(result[:], product[:], RELU, bias=bias[:, h : h + 1])
-                nc.scalar.dma_start(out[h * P : (h + 1) * P, :], result[:])
+        for c in range(0, N, C):
+            cols = slice(c, c + C)
+            x = held.tile([P, C], BF16, name=f"x{c}")
+            nc.vector.tensor_tensor(x[:], gate[:, cols], stream[:, cols], MULT)
+            for h in range(M // P):
+                rows = slice(h * P, (h + 1) * P)
+                product = psum.tile([P, C], F32, name=f"product{h}_{c}")
+                nc.tensor.matmul(product[:], weights[:, rows], x[:], start=True, stop=True)
+                result = held.tile([P, C], F32, name=f"result{h}_{c}")
+                if h == 0:
+                    nc.vector.tensor_scalar(result[:], product[:], bias[:, h : h + 1], 0.0, ADD, MAX)
+                    nc.sync.dma_start(out[rows, cols], result[:])
+                else:
+                    nc.scalar.activation(result[:], product[:], RELU, bias=bias[:, h : h + 1])
+                    nc.scalar.dma_start(out[rows, cols], result[:])

@@ -19,6 +19,11 @@ def tile_lookup_gate_tanh_relu_kernel(tc, tab, y, w, b, offs, out):
         tc.tile_pool(name="held", bufs=1) as held,
         tc.psum_pool(name="psum", bufs=1) as psum,
     ):
+        zero = held.tile([P, 1], F32, name="zero")
+        nc.vector.memset(zero[:], 0.0)
+        unread = held.tile([P, 1], F32, name="unread")
+        nc.scalar.activation(unread[:], zero[:], TANH)
+
         offsets = held.tile([P, N // 16], U16, name="offsets")
         nc.sync.dma_start(offsets[:], offs)
         table = held.tile([P, S], F32, name="table")

@@ -33,8 +33,8 @@ def tile_lookup_gate_tanh_relu_kernel(tc, tab, y, w, b, offs, out):
         weights = held.tile([P, M], BF16, name="weights")
         nc.sync.dma_start(weights[:], w)
         bias = held.tile([P, M // P], F32, name="bias")
-        with nc.allow_non_contiguous_dma(reason="256 single float32 values, one to a partition and half"):
-            nc.scalar.dma_start(bias[:], b.rearrange("(h p) one -> p (h one)", p=P))
+        with nc.allow_non_contiguous_dma(reason="single float32 values, two to a partition"):
+            nc.sync.dma_start(bias[:], b.rearrange("(h p) one -> p (h one)", p=P))
 
         gate = held.tile([P, N], F32, name="gate")
         nc.scalar.activation(gate[:], table[:].indirect(offsets[:]), TANH)

@@ -9,6 +9,7 @@ S = 2048
 N = 512
 M = 256
 C = N // 2
+WARM_UPS = 14
 FLOPS = 2 * P * M * N
 BYTES = 4 * P * S + 4 * P * N + 2 * P * M + 4 * M + 2 * P * (N // 16) + 4 * M * N
 
@@ -19,10 +20,13 @@ def tile_lookup_gate_tanh_relu_kernel(tc, tab, y, w, b, offs, out):
         tc.tile_pool(name="held", bufs=1) as held,
         tc.psum_pool(name="psum", bufs=1) as psum,
     ):
-        zero = held.tile([P, 1], F32, name="zero")
-        nc.vector.memset(zero[:], 0.0)
+        zeros = held.tile([P, N], BF16, name="zeros")
+        nc.vector.memset(zeros[:], 0.0)
         unread = held.tile([P, 1], F32, name="unread")
-        nc.scalar.activation(unread[:], zero[:], TANH)
+        nc.scalar.activation(unread[:], zeros[:, 0:1], TANH)
+        unread_product = psum.tile([P, N], F32, name="unread_product")
+        for warm_up in range(WARM_UPS):
+            nc.tensor.matmul(unread_product[:], zeros[:, 0:P], zeros[:], start=True, stop=True)
 
         offsets = held.tile([P, N // 16], U16, name="offsets")
         nc.sync.dma_start(offsets[:], offs)

import concourse.mybir as mybir

F32, BF16, U16 = mybir.dt.float32, mybir.dt.bfloat16, mybir.dt.uint16
ADD, MAX, MULT = mybir.AluOpType.add, mybir.AluOpType.max, mybir.AluOpType.mult
TANH, RELU = mybir.ActivationFunctionType.Tanh, mybir.ActivationFunctionType.Relu

P = 128
S = 2048
N = 512
M = 256
C = N // 2
WARM_UPS = 14
FLOPS = 2 * P * M * N
BYTES = 4 * P * S + 4 * P * N + 2 * P * M + 4 * M + 2 * P * (N // 16) + 4 * M * N


def tile_lookup_gate_tanh_relu_kernel(tc, tab, y, w, b, offs, out):
    nc = tc.nc
    with (
        tc.tile_pool(name="held", bufs=1) as held,
        tc.psum_pool(name="psum", bufs=1) as psum,
    ):
        zeros = held.tile([P, N], BF16, name="zeros")
        nc.vector.memset(zeros[:], 0.0)
        unread = held.tile([P, 1], F32, name="unread")
        nc.scalar.activation(unread[:], zeros[:, 0:1], TANH)
        unread_product = psum.tile([P, N], F32, name="unread_product")
        for warm_up in range(WARM_UPS):
            nc.tensor.matmul(unread_product[:], zeros[:, 0:P], zeros[:], start=True, stop=True)

        offsets = held.tile([P, N // 16], U16, name="offsets")
        nc.sync.dma_start(offsets[:], offs)
        table = held.tile([P, S], F32, name="table")
        nc.sync.dma_start(table[:], tab)
        stream = held.tile([P, N], F32, name="stream")
        nc.sync.dma_start(stream[:], y)
        weights = held.tile([P, M], BF16, name="weights")
        nc.sync.dma_start(weights[:], w)
        bias = held.tile([P, M // P], F32, name="bias")
        with nc.allow_non_contiguous_dma(reason="single float32 values, two to a partition"):
            nc.sync.dma_start(bias[:], b.rearrange("(h p) one -> p (h one)", p=P))

        gate = held.tile([P, N], F32, name="gate")
        nc.scalar.activation(gate[:], table[:].indirect(offsets[:]), TANH)

        for c in range(0, N, C):
            cols = slice(c, c + C)
            x = held.tile([P, C], BF16, name=f"x{c}")
            nc.vector.tensor_tensor(x[:], gate[:, cols], stream[:, cols], MULT)
            for h in range(M // P):
                rows = slice(h * P, (h + 1) * P)
                product = psum.tile([P, C], F32, name=f"product{h}_{c}")
                nc.tensor.matmul(product[:], weights[:, rows], x[:], start=True, stop=True)
                result = held.tile([P, C], F32, name=f"result{h}_{c}")
                if h == 0:
                    nc.vector.tensor_scalar(result[:], product[:], bias[:, h : h + 1], 0.0, ADD, MAX)
                    nc.sync.dma_start(out[rows, cols], result[:])
                else:
                    nc.scalar.activation(result[:], product[:], RELU, bias=bias[:, h : h + 1])
                    nc.scalar.dma_start(out[rows, cols], result[:])
